import numpy as np
import ml_dtypes


def mxq(x, axis, fmt="e4m3"):
    dtype, down = {"e4m3": (ml_dtypes.float8_e4m3fn, 7), "e5m2": (ml_dtypes.float8_e5m2, 14)}[fmt]
    v = np.moveaxis(np.asarray(x, np.float32).astype(ml_dtypes.bfloat16).astype(np.float64), axis, -1)
    blocks = v.reshape(v.shape[:-1] + (-1, 32))
    amax = np.abs(blocks).max(-1, keepdims=True)
    byte = np.maximum(np.where(amax > 0, np.frexp(amax)[1] - 1 + 127, 0) - down, 1)
    scale = np.exp2(byte - 127.0)
    codes = (blocks / scale).astype(np.float32).astype(dtype).astype(np.float64)
    return np.moveaxis((codes * scale).reshape(v.shape), -1, axis)


WIDE = False


def mx_kscale(k):
    if not WIDE:
        return np.ones(k)
    levels = np.array([10, -10, 5, -5, 0])
    if k % 512:
        return np.exp2(np.random.permutation(np.resize(levels, k // 32))).repeat(32)
    a = np.empty((k // 512, 16))
    for p in range(k // 512):
        a[p, :8] = np.random.permutation(np.resize(levels, 8))
        for g in range(8):
            far = levels[np.abs(levels - a[p, g]) >= 10]
            a[p, g + 8] = far[np.random.randint(len(far))]
    return np.exp2(a.ravel()).repeat(32)


def f64(x):
    return np.asarray(x).astype(np.float64)


def striped(idx):
    return np.tile(np.asarray(idx).reshape(-1, 16).T, (8, 1)).astype(np.uint16)


def unstriped(offs):
    return offs[:16].T.reshape(-1).astype(np.int64)


def rot(x):
    y = x.reshape(-1, 2, x.shape[1])
    return np.stack([-y[:, 1], y[:, 0]], axis=1).reshape(x.shape)


D, T, I, U, Q = 512, 1024, 512, 1024, 256


def setup_inputs():
    n = np.random.standard_normal
    idx = np.random.permutation(T)[:I]
    idx2 = np.random.permutation(T)[:I]
    idx3 = np.random.randint(0, U, I)
    fd = mx_kscale(D)
    return {
        "query": (n((D, Q)) * 0.8 / np.sqrt(D) * fd[:, None]).astype(np.float32),
        "keys": (n((D, T)) / fd[:, None]).astype(np.float32),
        "cosn": (np.repeat(np.round(np.cos(np.arange(D // 2)[:, None] * 0.11 + np.arange(U)[None] * 0.37) * 64) / 64, 2, axis=0)).astype(np.float32),
        "sinn": (np.repeat(np.round(np.sin(np.arange(D // 2)[:, None] * 0.11 + np.arange(U)[None] * 0.37) * 64) / 64, 2, axis=0)).astype(np.float32),
        "ka": (np.random.uniform(0.4, 0.8, (1, I))).astype(np.float32),
        "kb": (np.random.uniform(0.3, 0.7, (1, I))).astype(np.float32),
        "offs": striped(idx),
        "offs2": striped(idx2),
        "offs3": striped(idx3),
    }


def reference(query, keys, cosn, sinn, ka, kb, offs, offs2, offs3):
    idx = unstriped(offs)
    idx2 = unstriped(offs2)
    idx3 = unstriped(offs3)
    kr = rot(f64(keys)[:, idx2])
    k2 = f64(keys)[:, idx2] * f64(cosn)[:, idx3] + kr * f64(sinn)[:, idx3]
    km = f64(keys)[:, idx] * f64(ka) + k2 * f64(kb)
    queryq = mxq(f64(query), 0, "e4m3")
    kmq = mxq(km, 0, "e4m3")
    a = queryq.T @ kmq
    p = np.exp(a - np.max(a, axis=1, keepdims=True))
    y = p / np.sum(p, axis=1, keepdims=True) * 512.0
    return y

@@ -1,0 +1,187 @@
+from contextlib import ExitStack
+
+import concourse.mybir as mybir
+from concourse.masks import make_identity
+
+D, T, I, U, Q = 512, 1024, 512, 1024, 256
+FLOPS = 2 * D * Q * I
+BYTES = 4 * (D * Q + D * T + D * U + 2 * I + Q * I) + 3 * 128 * 32 * 2
+
+F32 = mybir.dt.float32
+BF16 = mybir.dt.bfloat16
+U32 = mybir.dt.uint32
+U16 = mybir.dt.uint16
+U8 = mybir.dt.uint8
+FP8X4 = mybir.dt.float8_e4m3fn_x4
+ALU = mybir.AluOpType
+ACT = mybir.ActivationFunctionType
+P = 128
+NB = I // P
+ND = 2
+NP = NB - ND
+
+
+def tile_attend_ropemerge_kernel(tc, query, keys, cosn, sinn, ka, kb, offs, offs2, offs3, out):
+    nc = tc.nc
+    with ExitStack() as ctx:
+        lists = ctx.enter_context(tc.tile_pool(name="lists", bufs=1))
+        sb = ctx.enter_context(tc.tile_pool(name="sb", bufs=1))
+        ps = ctx.enter_context(tc.psum_pool(name="ps", bufs=1))
+
+        def bank(tag):
+            return ps.tile([P, 512], F32, tag=tag, name=tag)
+
+        def turn(dst, src, start, stop):
+            nc.tensor.matmul(dst, lhsT=src, rhs=ident[:], is_transpose=True, start=start, stop=stop)
+
+        o1 = lists.tile([P, I // 16], U16, name="o1")
+        o2 = lists.tile([P, I // 16], U16, name="o2")
+        o3 = lists.tile([P, I // 16], U16, name="o3")
+        kpl = [sb.tile([P, T], F32, name="kpl%d" % t) for t in range(4)]
+        cpl = [sb.tile([P, U], F32, name="cpl%d" % u) for u in range(2)]
+        spl = [sb.tile([P, U], F32, name="spl%d" % u) for u in range(2)]
+        qraw = sb.tile([P, 4, Q], F32, name="qraw")
+        kv = keys.rearrange("(p t) n -> p t n", t=4)
+        cv = cosn.rearrange("(p t) n -> p t n", t=4)
+        sv = sinn.rearrange("(p t) n -> p t n", t=4)
+
+        rows = sb.tile([P, P], F32, name="rows")
+        nc.vector.memset(rows[:], 0.0)
+        nc.scalar.dma_start(out=rows[0:NB, :], in_=ka.rearrange("o (j p) -> (o j) p", p=P))
+        nc.scalar.dma_start(out=rows[NB : 2 * NB, :], in_=kb.rearrange("o (j p) -> (o j) p", p=P))
+        warm = sb.tile([P, 1], F32, name="warm")
+        zero = sb.tile([P, 1], F32, name="zero")
+        nc.vector.memset(zero[:], 0.0)
+        nc.scalar.activation(out=warm[:], in_=zero[:], func=ACT.Exp)
+
+        nc.sync.dma_start(o2[:], offs2)
+        nc.sync.dma_start(out=kpl[0][:], in_=kv[:, 0, :])
+        nc.sync.dma_start(o3[:], offs3)
+        nc.sync.dma_start(out=cpl[0][:], in_=cv[:, 0, :])
+        nc.sync.dma_start(out=kpl[1][:], in_=kv[:, 1, :])
+        nc.sync.dma_start(out=spl[0][:], in_=sv[:, 0, :])
+        nc.sync.dma_start(out=kpl[2][:], in_=kv[:, 2, :])
+        nc.sync.dma_start(out=cpl[1][:], in_=cv[:, 2, :])
+        nc.sync.dma_start(out=kpl[3][:], in_=kv[:, 3, :])
+        nc.sync.dma_start(out=spl[1][:], in_=sv[:, 2, :])
+        nc.sync.dma_start(o1[:], offs)
+        nc.sync.dma_start(out=qraw[:], in_=query.rearrange("(p t) q -> p t q", t=4))
+
+        ident = sb.tile([P, P], F32, name="ident")
+        make_identity(nc, ident[:])
+
+        b0 = bank("sc0")
+        turn(b0[:, 0:P], rows[:], True, True)
+        share = sb.tile([P, 2 * NB], F32, name="share")
+        nc.scalar.copy(out=share[:], in_=b0[:, 0 : 2 * NB])
+        b1 = bank("sc1")
+        for j in range(NP, NB):
+            turn(b1[:, (j - NP) * P : (j - NP + 1) * P], share[:, j : j + 1].to_broadcast([P, P]), True, True)
+        kab = sb.tile([P, ND * P], F32, name="kab")
+        nc.scalar.copy(out=kab[:], in_=b1[:, 0 : ND * P])
+
+        fin = [bank("fin%d" % j) for j in range(NB)]
+        half0 = sb.tile([P, Q + 2 * P, 4], BF16, name="half0", align_bytes=64)
+        half1 = sb.tile([P, 2 * P, 4], BF16, name="half1", align_bytes=64)
+
+        def km16(j):
+            return half0[:, Q + j * P : Q + (j + 1) * P, :] if j < 2 else half1[:, (j - 2) * P : (j - 1) * P, :]
+
+        def rotate(u, tags):
+            g = sb.tile([P, 3, I], F32, name="g%d" % u)
+            cg = sb.tile([P, I], F32, name="cg%d" % u)
+            sg = sb.tile([P, I], F32, name="sg%d" % u)
+            pc = sb.tile([P, 2, I], F32, name="pc%d" % u)
+            pq = [sb.tile([P, 2, I // 2], F32, name="pq%d_%d" % (u, h)) for h in range(2)]
+            nc.vector.tensor_copy(g[:, 1, :], kpl[2 * u][:].indirect(o2[:]))
+            nc.vector.tensor_copy(cg[:], cpl[u][:].indirect(o3[:]))
+            nc.vector.tensor_copy(g[:, 2, :], kpl[2 * u + 1][:].indirect(o2[:]))
+            nc.vector.tensor_copy(sg[:], spl[u][:].indirect(o3[:]))
+            nc.scalar.activation(out=g[:, 0, :], in_=g[:, 2, :], func=ACT.Copy, scale=-1.0)
+            for e in range(2):
+                nc.gpsimd.tensor_tensor(pc[:, e, :], g[:, 1 + e, :], cg[:], ALU.mult)
+            for h in range(2):
+                cols = slice(h * 256, (h + 1) * 256)
+                nc.gpsimd.tensor_tensor(pq[h][:], g[:, 0:2, cols], sg[:, cols].unsqueeze(1).to_broadcast([P, 2, 256]), ALU.mult)
+            for h in range(2):
+                fw = bank(tags[h])
+                for e in range(2):
+                    for jj in range(2):
+                        j = 2 * h + jj
+                        turn(fw[:, (2 * jj + e) * P : (2 * jj + e + 1) * P], pc[:, e, j * P : (j + 1) * P], e == 0 and jj == 0, False)
+                for e in range(2):
+                    for jj in range(2):
+                        turn(fw[:, (2 * jj + e) * P : (2 * jj + e + 1) * P], pq[h][:, e, jj * P : (jj + 1) * P], False, e == 1 and jj == 1)
+                for jj in range(2):
+                    j = 2 * h + jj
+                    bt = sb.tile([P, 2 * P], F32, name="bt%d_%d" % (u, j))
+                    nc.scalar.activation(out=bt[:], in_=fw[:, jj * 256 : (jj + 1) * 256], func=ACT.Copy, scale=share[:, NB + j : NB + j + 1])
+                    for e in range(2):
+                        t = 2 * u + e
+                        turn(fin[j][:, t * P : (t + 1) * P], bt[:, e * P : (e + 1) * P], t == 0, t == 3 and j >= NP)
+
+        rotate(0, ["fwA", "fwB"])
+        rotate(1, ["sc0", "sc1"])
+
+        nc.scalar.copy(
+            out=half0[:, 0:Q, :].rearrange("p (c i) t -> p c t i", i=4),
+            in_=qraw[:].rearrange("p t (c i) -> p c t i", i=4),
+        )
+
+        pieces = [[0,2]]
+        for (j0, j1) in pieces:
+            n = (j1 - j0) * P
+            ga = sb.tile([P, 4, n], F32, name="ga%d" % j0)
+            for t in range(4):
+                nc.vector.tensor_copy(ga[:, t, :], kpl[t][:].indirect(o1[:, j0 * 8 : j1 * 8]))
+            for j in range(j0, j1):
+                fw = bank("fwA" if j % 2 == 0 else "fwB")
+                for t in range(4):
+                    turn(fw[:, t * P : (t + 1) * P], ga[:, t, (j - j0) * P : (j - j0 + 1) * P], True, True)
+                at = sb.tile([P, 4 * P], F32, name="at%d" % j)
+                nc.scalar.activation(out=at[:], in_=fw[:], func=ACT.Copy, scale=share[:, j : j + 1])
+                for t in range(4):
+                    turn(fin[j][:, t * P : (t + 1) * P], at[:, t * P : (t + 1) * P], False, t == 3)
+                nc.scalar.copy(out=km16(j), in_=fin[j][:].rearrange("p (t s) -> p s t", t=4))
+        gd = sb.tile([P, 4, ND * P], F32, name="gd")
+        for t in range(4):
+            nc.vector.tensor_tensor(gd[:, t, :], kpl[t][:].indirect(o1[:, NP * 8 : NB * 8]), kab[:], ALU.mult)
+        for j in range(NP, NB):
+            nc.vector.tensor_tensor(
+                km16(j).rearrange("p (c i) t -> p c t i", i=4),
+                fin[j][:].rearrange("p (t c i) -> p c t i", t=4, i=4),
+                gd[:, :, (j - NP) * P : (j - NP + 1) * P].rearrange("p t (c i) -> p c t i", i=4),
+                ALU.add,
+            )
+
+        c0 = sb.tile([P, Q + 2 * P], U32, name="c0", align_bytes=64)
+        s0 = sb.tile([P, Q + 2 * P], U8, name="s0", align_bytes=64)
+        c1 = sb.tile([P, 2 * P], U32, name="c1", align_bytes=64)
+        s1 = sb.tile([P, 2 * P], U8, name="s1", align_bytes=64)
+        nc.vector.quantize_mx(out=c0[:].bitcast(FP8X4), scales=s0[:], in_=half0[:].rearrange("p s t -> p (s t)"))
+        nc.vector.quantize_mx(out=c1[:].bitcast(FP8X4), scales=s1[:], in_=half1[:].rearrange("p s t -> p (s t)"))
+
+        score = [bank("sc%d" % m) for m in range(2)]
+        for h in range(2):
+            for m in range(2):
+                rc, rs = (c0[:, Q:], s0[:, Q:]) if h == 0 else (c1[:], s1[:])
+                nc.tensor.matmul_mx(
+                    out=score[m][:, h * 256 : (h + 1) * 256],
+                    lhsT=c0[:, m * P : (m + 1) * P].bitcast(FP8X4),
+                    lhsT_scale=s0[:, m * P : (m + 1) * P],
+                    rhs=rc.bitcast(FP8X4),
+                    rhs_scale=rs,
+                    start=True,
+                    stop=True,
+                )
+        for m in range(2):
+            nmax = sb.tile([P, 1], F32, name="nmax%d" % m)
+            nc.vector.tensor_reduce(out=nmax[:], in_=score[m][:], axis=mybir.AxisListType.X, op=ALU.max, negate=True)
+            p = sb.tile([P, I], F32, name="p%d" % m)
+            total = sb.tile([P, 1], F32, name="total%d" % m)
+            nc.scalar.activation(out=p[:], in_=score[m][:], func=ACT.Exp, bias=nmax[:], scale=1.0, accum_out=total[:])
+            inv = sb.tile([P, 1], F32, name="inv%d" % m)
+            nc.vector.reciprocal(out=inv[:], in_=total[:])
+            y = sb.tile([P, I], F32, name="y%d" % m)
+            nc.vector.tensor_scalar(out=y[:], in0=p[:], scalar1=inv[:], scalar2=512.0, op0=ALU.mult, op1=ALU.mult)
+            nc.sync.dma_start(out=out[m * P : (m + 1) * P, :], in_=y[:])

@@ -5,7 +5,7 @@ from concourse.masks import make_identity
 
 D, T, I, U, Q = 512, 1024, 512, 1024, 256
 FLOPS = 2 * D * Q * I
-BYTES = 4 * (D * Q + D * T + D * U + 2 * I + Q * I) + 3 * 128 * 32 * 2
+BYTES = 4 * (D * Q + D * T + D * U + 2 * I + Q * I) + 3 * 128 * (I // 16) * 2
 
 F32 = mybir.dt.float32
 BF16 = mybir.dt.bfloat16
@@ -15,10 +15,21 @@ U8 = mybir.dt.uint8
 FP8X4 = mybir.dt.float8_e4m3fn_x4
 ALU = mybir.AluOpType
 ACT = mybir.ActivationFunctionType
+
 P = 128
-NB = I // P
-ND = 2
-NP = NB - ND
+PLANES = 4
+BLOCKS = I // P
+HALF = I // 2
+BANK = 512
+RUN = 4
+
+
+def cols(k):
+    return slice(k * P, (k + 1) * P)
+
+
+def by_feature(turned, jj):
+    return turned[:, jj * 2 * P : (jj + 1) * 2 * P].rearrange("s (e p) -> s p e", e=2)
 
 
 def tile_attend_ropemerge_kernel(tc, query, keys, cosn, sinn, ka, kb, offs, offs2, offs3, out):
@@ -28,160 +39,160 @@ def tile_attend_ropemerge_kernel(tc, query, keys, cosn, sinn, ka, kb, offs, offs
         sb = ctx.enter_context(tc.tile_pool(name="sb", bufs=1))
         ps = ctx.enter_context(tc.psum_pool(name="ps", bufs=1))
 
-        def bank(tag):
-            return ps.tile([P, 512], F32, tag=tag, name=tag)
+        def bank(n):
+            return ps.tile([P, BANK], F32, tag="bank%d" % n, name="bank%d" % n)
 
         def turn(dst, src, start, stop):
             nc.tensor.matmul(dst, lhsT=src, rhs=ident[:], is_transpose=True, start=start, stop=stop)
 
-        o1 = lists.tile([P, I // 16], U16, name="o1")
-        o2 = lists.tile([P, I // 16], U16, name="o2")
-        o3 = lists.tile([P, I // 16], U16, name="o3")
-        kpl = [sb.tile([P, T], F32, name="kpl%d" % t) for t in range(4)]
-        cpl = [sb.tile([P, U], F32, name="cpl%d" % u) for u in range(2)]
-        spl = [sb.tile([P, U], F32, name="spl%d" % u) for u in range(2)]
-        qraw = sb.tile([P, 4, Q], F32, name="qraw")
-        kv = keys.rearrange("(p t) n -> p t n", t=4)
-        cv = cosn.rearrange("(p t) n -> p t n", t=4)
-        sv = sinn.rearrange("(p t) n -> p t n", t=4)
+        list1 = lists.tile([P, I // 16], U16, name="list1")
+        list2 = lists.tile([P, I // 16], U16, name="list2")
+        list3 = lists.tile([P, I // 16], U16, name="list3")
+        key_plane = [sb.tile([P, T], F32, name="key_plane%d" % t) for t in range(PLANES)]
+        cos_rows = [sb.tile([P, U], F32, name="cos_rows%d" % u) for u in range(2)]
+        sin_rows = [sb.tile([P, U], F32, name="sin_rows%d" % u) for u in range(2)]
+        query_raw = sb.tile([P, PLANES, Q], F32, name="query_raw")
+        keys_by_plane = keys.rearrange("(p t) n -> p t n", t=PLANES)
+        cos_by_plane = cosn.rearrange("(p t) n -> p t n", t=PLANES)
+        sin_by_plane = sinn.rearrange("(p t) n -> p t n", t=PLANES)
 
-        rows = sb.tile([P, P], F32, name="rows")
-        nc.vector.memset(rows[:], 0.0)
-        nc.scalar.dma_start(out=rows[0:NB, :], in_=ka.rearrange("o (j p) -> (o j) p", p=P))
-        nc.scalar.dma_start(out=rows[NB : 2 * NB, :], in_=kb.rearrange("o (j p) -> (o j) p", p=P))
-        warm = sb.tile([P, 1], F32, name="warm")
-        zero = sb.tile([P, 1], F32, name="zero")
-        nc.vector.memset(zero[:], 0.0)
-        nc.scalar.activation(out=warm[:], in_=zero[:], func=ACT.Exp)
+        share_rows = sb.tile([P, P], F32, name="share_rows")
+        nc.vector.memset(share_rows[:], 0.0)
+        nc.scalar.dma_start(out=share_rows[0:BLOCKS, :], in_=ka.rearrange("o (j p) -> (o j) p", p=P))
+        nc.scalar.dma_start(out=share_rows[BLOCKS : 2 * BLOCKS, :], in_=kb.rearrange("o (j p) -> (o j) p", p=P))
 
-        nc.sync.dma_start(o2[:], offs2)
-        nc.sync.dma_start(out=kpl[0][:], in_=kv[:, 0, :])
-        nc.sync.dma_start(o3[:], offs3)
-        nc.sync.dma_start(out=cpl[0][:], in_=cv[:, 0, :])
-        nc.sync.dma_start(out=kpl[1][:], in_=kv[:, 1, :])
-        nc.sync.dma_start(out=spl[0][:], in_=sv[:, 0, :])
-        nc.sync.dma_start(out=kpl[2][:], in_=kv[:, 2, :])
-        nc.sync.dma_start(out=cpl[1][:], in_=cv[:, 2, :])
-        nc.sync.dma_start(out=kpl[3][:], in_=kv[:, 3, :])
-        nc.sync.dma_start(out=spl[1][:], in_=sv[:, 2, :])
-        nc.sync.dma_start(o1[:], offs)
-        nc.sync.dma_start(out=qraw[:], in_=query.rearrange("(p t) q -> p t q", t=4))
+        nc.sync.dma_start(list2[:], offs2)
+        nc.sync.dma_start(out=key_plane[0][:], in_=keys_by_plane[:, 0, :])
+        nc.sync.dma_start(list3[:], offs3)
+        nc.sync.dma_start(out=cos_rows[0][:], in_=cos_by_plane[:, 0, :])
+        nc.sync.dma_start(out=key_plane[1][:], in_=keys_by_plane[:, 1, :])
+        nc.sync.dma_start(out=sin_rows[0][:], in_=sin_by_plane[:, 0, :])
+        nc.sync.dma_start(out=key_plane[2][:], in_=keys_by_plane[:, 2, :])
+        nc.sync.dma_start(out=cos_rows[1][:], in_=cos_by_plane[:, 2, :])
+        nc.sync.dma_start(out=key_plane[3][:], in_=keys_by_plane[:, 3, :])
+        nc.sync.dma_start(out=sin_rows[1][:], in_=sin_by_plane[:, 2, :])
+        nc.sync.dma_start(list1[:], offs)
+        nc.sync.dma_start(out=query_raw[:], in_=query.rearrange("(p t) q -> p t q", t=PLANES))
 
         ident = sb.tile([P, P], F32, name="ident")
         make_identity(nc, ident[:])
 
-        b0 = bank("sc0")
-        turn(b0[:, 0:P], rows[:], True, True)
-        share = sb.tile([P, 2 * NB], F32, name="share")
-        nc.scalar.copy(out=share[:], in_=b0[:, 0 : 2 * NB])
-        b1 = bank("sc1")
-        for j in range(NP, NB):
-            turn(b1[:, (j - NP) * P : (j - NP + 1) * P], share[:, j : j + 1].to_broadcast([P, P]), True, True)
-        kab = sb.tile([P, ND * P], F32, name="kab")
-        nc.scalar.copy(out=kab[:], in_=b1[:, 0 : ND * P])
+        share_turned = bank(6)
+        turn(share_turned[:, 0:P], share_rows[:], True, True)
+        share = sb.tile([P, 2 * BLOCKS], F32, name="share")
+        nc.scalar.copy(out=share[:], in_=share_turned[:, 0 : 2 * BLOCKS])
 
-        fin = [bank("fin%d" % j) for j in range(NB)]
-        half0 = sb.tile([P, Q + 2 * P, 4], BF16, name="half0", align_bytes=64)
-        half1 = sb.tile([P, 2 * P, 4], BF16, name="half1", align_bytes=64)
+        km16 = [sb.tile([P, HALF, PLANES], BF16, name="km16_%d" % h, align_bytes=64) for h in range(2)]
+        query16 = sb.tile([P, Q, PLANES], BF16, name="query16", align_bytes=64)
 
-        def km16(j):
-            return half0[:, Q + j * P : Q + (j + 1) * P, :] if j < 2 else half1[:, (j - 2) * P : (j - 1) * P, :]
-
-        def rotate(u, tags):
-            g = sb.tile([P, 3, I], F32, name="g%d" % u)
-            cg = sb.tile([P, I], F32, name="cg%d" % u)
-            sg = sb.tile([P, I], F32, name="sg%d" % u)
-            pc = sb.tile([P, 2, I], F32, name="pc%d" % u)
-            pq = [sb.tile([P, 2, I // 2], F32, name="pq%d_%d" % (u, h)) for h in range(2)]
-            nc.vector.tensor_copy(g[:, 1, :], kpl[2 * u][:].indirect(o2[:]))
-            nc.vector.tensor_copy(cg[:], cpl[u][:].indirect(o3[:]))
-            nc.vector.tensor_copy(g[:, 2, :], kpl[2 * u + 1][:].indirect(o2[:]))
-            nc.vector.tensor_copy(sg[:], spl[u][:].indirect(o3[:]))
-            nc.scalar.activation(out=g[:, 0, :], in_=g[:, 2, :], func=ACT.Copy, scale=-1.0)
+        rotated = {}
+        for u in range(2):
+            second = sb.tile([P, 3, I], F32, name="second%d" % u)
+            cos = sb.tile([P, I], F32, name="cos%d" % u)
+            sin = sb.tile([P, I], F32, name="sin%d" % u)
+            by_cos = sb.tile([P, 2, I], F32, name="by_cos%d" % u)
+            by_sin = [sb.tile([P, 2, HALF], F32, name="by_sin%d_%d" % (u, h)) for h in range(2)]
+            nc.vector.tensor_copy(second[:, 1, :], key_plane[2 * u][:].indirect(list2[:]))
+            nc.vector.tensor_copy(cos[:], cos_rows[u][:].indirect(list3[:]))
+            nc.vector.tensor_copy(second[:, 2, :], key_plane[2 * u + 1][:].indirect(list2[:]))
+            nc.vector.tensor_copy(sin[:], sin_rows[u][:].indirect(list3[:]))
+            nc.scalar.activation(out=second[:, 0, :], in_=second[:, 2, :], func=ACT.Copy, scale=-1.0)
             for e in range(2):
-                nc.gpsimd.tensor_tensor(pc[:, e, :], g[:, 1 + e, :], cg[:], ALU.mult)
+                nc.gpsimd.tensor_tensor(by_cos[:, e, :], second[:, 1 + e, :], cos[:], ALU.mult)
             for h in range(2):
-                cols = slice(h * 256, (h + 1) * 256)
-                nc.gpsimd.tensor_tensor(pq[h][:], g[:, 0:2, cols], sg[:, cols].unsqueeze(1).to_broadcast([P, 2, 256]), ALU.mult)
+                slots = slice(h * HALF, (h + 1) * HALF)
+                sin_both = sin[:, slots].unsqueeze(1).to_broadcast([P, 2, HALF])
+                nc.gpsimd.tensor_tensor(by_sin[h][:], second[:, 0:2, slots], sin_both, ALU.mult)
+            k2_turned = [bank(2 * u + h) for h in range(2)]
+            for e in range(2):
+                for j in range(BLOCKS):
+                    h, jj = divmod(j, 2)
+                    turn(k2_turned[h][:, cols(2 * jj + e)], by_cos[:, e, cols(j)], e == 0 and jj == 0, False)
             for h in range(2):
-                fw = bank(tags[h])
                 for e in range(2):
                     for jj in range(2):
-                        j = 2 * h + jj
-                        turn(fw[:, (2 * jj + e) * P : (2 * jj + e + 1) * P], pc[:, e, j * P : (j + 1) * P], e == 0 and jj == 0, False)
-                for e in range(2):
-                    for jj in range(2):
-                        turn(fw[:, (2 * jj + e) * P : (2 * jj + e + 1) * P], pq[h][:, e, jj * P : (jj + 1) * P], False, e == 1 and jj == 1)
+                        turn(k2_turned[h][:, cols(2 * jj + e)], by_sin[h][:, e, cols(jj)], False, e == 1 and jj == 1)
                 for jj in range(2):
                     j = 2 * h + jj
-                    bt = sb.tile([P, 2 * P], F32, name="bt%d_%d" % (u, j))
-                    nc.scalar.activation(out=bt[:], in_=fw[:, jj * 256 : (jj + 1) * 256], func=ACT.Copy, scale=share[:, NB + j : NB + j + 1])
-                    for e in range(2):
-                        t = 2 * u + e
-                        turn(fin[j][:, t * P : (t + 1) * P], bt[:, e * P : (e + 1) * P], t == 0, t == 3 and j >= NP)
-
-        rotate(0, ["fwA", "fwB"])
-        rotate(1, ["sc0", "sc1"])
+                    tag = "rotated%d_%d" % (u, j)
+                    rotated[u, j] = sb.tile([P, P, 2], F32, name=tag, tag=tag, align_bytes=64)
+                    nc.scalar.activation(
+                        out=rotated[u, j][:],
+                        in_=by_feature(k2_turned[h], jj),
+                        func=ACT.Copy,
+                        scale=share[:, BLOCKS + j : BLOCKS + j + 1],
+                    )
 
         nc.scalar.copy(
-            out=half0[:, 0:Q, :].rearrange("p (c i) t -> p c t i", i=4),
-            in_=qraw[:].rearrange("p t (c i) -> p c t i", i=4),
+            out=query16[:].rearrange("p (c i) t -> p c t i", i=RUN),
+            in_=query_raw[:].rearrange("p t (c i) -> p c t i", i=RUN),
         )
 
-        pieces = [[0,2]]
-        for (j0, j1) in pieces:
-            n = (j1 - j0) * P
-            ga = sb.tile([P, 4, n], F32, name="ga%d" % j0)
-            for t in range(4):
-                nc.vector.tensor_copy(ga[:, t, :], kpl[t][:].indirect(o1[:, j0 * 8 : j1 * 8]))
-            for j in range(j0, j1):
-                fw = bank("fwA" if j % 2 == 0 else "fwB")
-                for t in range(4):
-                    turn(fw[:, t * P : (t + 1) * P], ga[:, t, (j - j0) * P : (j - j0 + 1) * P], True, True)
-                at = sb.tile([P, 4 * P], F32, name="at%d" % j)
-                nc.scalar.activation(out=at[:], in_=fw[:], func=ACT.Copy, scale=share[:, j : j + 1])
-                for t in range(4):
-                    turn(fin[j][:, t * P : (t + 1) * P], at[:, t * P : (t + 1) * P], False, t == 3)
-                nc.scalar.copy(out=km16(j), in_=fin[j][:].rearrange("p (t s) -> p s t", t=4))
-        gd = sb.tile([P, 4, ND * P], F32, name="gd")
-        for t in range(4):
-            nc.vector.tensor_tensor(gd[:, t, :], kpl[t][:].indirect(o1[:, NP * 8 : NB * 8]), kab[:], ALU.mult)
-        for j in range(NP, NB):
-            nc.vector.tensor_tensor(
-                km16(j).rearrange("p (c i) t -> p c t i", i=4),
-                fin[j][:].rearrange("p (t c i) -> p c t i", t=4, i=4),
-                gd[:, :, (j - NP) * P : (j - NP + 1) * P].rearrange("p t (c i) -> p c t i", i=4),
-                ALU.add,
+        k1_turned = {}
+        for u in range(2):
+            first = sb.tile([P, 2, I], F32, name="first%d" % u)
+            for h in range(2):
+                k1_turned[u, h] = bank(4 - 2 * u + h)
+            for e in range(2):
+                nc.vector.tensor_copy(first[:, e, :], key_plane[2 * u + e][:].indirect(list1[:]))
+                for j in range(BLOCKS):
+                    h, jj = divmod(j, 2)
+                    turn(k1_turned[u, h][:, cols(2 * jj + e)], first[:, e, cols(j)], True, True)
+
+        words = [bank(n) for n in (0, 1, 6, 7)]
+        for u in range(2):
+            for j in range(BLOCKS):
+                h, jj = divmod(j, 2)
+                merged = sb.tile([P, P, 2], BF16, name="merged%d_%d" % (u, j))
+                nc.vector.scalar_tensor_tensor(
+                    merged[:], by_feature(k1_turned[u, h], jj), share[:, j : j + 1], rotated[u, j][:], ALU.mult, ALU.add
+                )
+                turn(words[j][:, cols(u)], merged[:].rearrange("s p e -> s (p e)").bitcast(F32), True, True)
+        for j in range(BLOCKS):
+            h, jj = divmod(j, 2)
+            block16 = km16[h][:, cols(jj), :].rearrange("p s t -> p (s t)")
+            nc.scalar.copy(
+                out=block16.bitcast(F32).rearrange("p (s u) -> p s u", u=2),
+                in_=words[j][:, 0 : 2 * P].rearrange("p (u s) -> p s u", u=2),
             )
 
-        c0 = sb.tile([P, Q + 2 * P], U32, name="c0", align_bytes=64)
-        s0 = sb.tile([P, Q + 2 * P], U8, name="s0", align_bytes=64)
-        c1 = sb.tile([P, 2 * P], U32, name="c1", align_bytes=64)
-        s1 = sb.tile([P, 2 * P], U8, name="s1", align_bytes=64)
-        nc.vector.quantize_mx(out=c0[:].bitcast(FP8X4), scales=s0[:], in_=half0[:].rearrange("p s t -> p (s t)"))
-        nc.vector.quantize_mx(out=c1[:].bitcast(FP8X4), scales=s1[:], in_=half1[:].rearrange("p s t -> p (s t)"))
-
-        score = [bank("sc%d" % m) for m in range(2)]
+        query_codes = sb.tile([P, Q], U32, name="query_codes", tag="rotated1_%d" % (BLOCKS - 1), align_bytes=64)
+        query_scales = sb.tile([P, Q], U8, name="query_scales", align_bytes=64)
+        nc.vector.quantize_mx(
+            out=query_codes[:].bitcast(FP8X4), scales=query_scales[:], in_=query16[:].rearrange("p s t -> p (s t)")
+        )
+        km_codes = [sb.tile([P, HALF], U32, name="km_codes%d" % h, align_bytes=64) for h in range(2)]
+        km_scales = [sb.tile([P, HALF], U8, name="km_scales%d" % h, align_bytes=64) for h in range(2)]
         for h in range(2):
-            for m in range(2):
-                rc, rs = (c0[:, Q:], s0[:, Q:]) if h == 0 else (c1[:], s1[:])
+            nc.vector.quantize_mx(
+                out=km_codes[h][:].bitcast(FP8X4), scales=km_scales[h][:], in_=km16[h][:].rearrange("p s t -> p (s t)")
+            )
+
+        score = [bank(4 + m) for m in range(Q // P)]
+        for h in range(2):
+            for m in range(Q // P):
                 nc.tensor.matmul_mx(
-                    out=score[m][:, h * 256 : (h + 1) * 256],
-                    lhsT=c0[:, m * P : (m + 1) * P].bitcast(FP8X4),
-                    lhsT_scale=s0[:, m * P : (m + 1) * P],
-                    rhs=rc.bitcast(FP8X4),
-                    rhs_scale=rs,
+                    out=score[m][:, h * HALF : (h + 1) * HALF],
+                    lhsT=query_codes[:, cols(m)].bitcast(FP8X4),
+                    lhsT_scale=query_scales[:, cols(m)],
+                    rhs=km_codes[h][:].bitcast(FP8X4),
+                    rhs_scale=km_scales[h][:],
                     start=True,
                     stop=True,
                 )
-        for m in range(2):
-            nmax = sb.tile([P, 1], F32, name="nmax%d" % m)
-            nc.vector.tensor_reduce(out=nmax[:], in_=score[m][:], axis=mybir.AxisListType.X, op=ALU.max, negate=True)
-            p = sb.tile([P, I], F32, name="p%d" % m)
+
+        for m in range(Q // P):
+            neg_max = sb.tile([P, 1], F32, name="neg_max%d" % m)
+            nc.vector.tensor_reduce(out=neg_max[:], in_=score[m][:], axis=mybir.AxisListType.X, op=ALU.max, negate=True)
+            weight = sb.tile([P, I], F32, name="weight%d" % m)
             total = sb.tile([P, 1], F32, name="total%d" % m)
-            nc.scalar.activation(out=p[:], in_=score[m][:], func=ACT.Exp, bias=nmax[:], scale=1.0, accum_out=total[:])
-            inv = sb.tile([P, 1], F32, name="inv%d" % m)
-            nc.vector.reciprocal(out=inv[:], in_=total[:])
-            y = sb.tile([P, I], F32, name="y%d" % m)
-            nc.vector.tensor_scalar(out=y[:], in0=p[:], scalar1=inv[:], scalar2=512.0, op0=ALU.mult, op1=ALU.mult)
-            nc.sync.dma_start(out=out[m * P : (m + 1) * P, :], in_=y[:])
+            nc.scalar.activation(
+                out=weight[:], in_=score[m][:], func=ACT.Exp, bias=neg_max[:], scale=1.0, accum_out=total[:]
+            )
+            inverse = sb.tile([P, 1], F32, name="inverse%d" % m)
+            nc.vector.reciprocal(out=inverse[:], in_=total[:])
+            result = sb.tile([P, I], F32, name="result%d" % m)
+            nc.vector.tensor_scalar(
+                out=result[:], in0=weight[:], scalar1=inverse[:], scalar2=512.0, op0=ALU.mult, op1=ALU.mult
+            )
+            nc.sync.dma_start(out=out[cols(m), :], in_=result[:])

from contextlib import ExitStack

import concourse.mybir as mybir
from concourse.masks import make_identity

D, T, I, U, Q = 512, 1024, 512, 1024, 256
FLOPS = 2 * D * Q * I
BYTES = 4 * (D * Q + D * T + D * U + 2 * I + Q * I) + 3 * 128 * (I // 16) * 2

F32 = mybir.dt.float32
BF16 = mybir.dt.bfloat16
U32 = mybir.dt.uint32
U16 = mybir.dt.uint16
U8 = mybir.dt.uint8
FP8X4 = mybir.dt.float8_e4m3fn_x4
ALU = mybir.AluOpType
ACT = mybir.ActivationFunctionType

P = 128
PLANES = 4
BLOCKS = I // P
HALF = I // 2
BANK = 512
RUN = 4


def cols(k):
    return slice(k * P, (k + 1) * P)


def by_feature(turned, jj):
    return turned[:, jj * 2 * P : (jj + 1) * 2 * P].rearrange("s (e p) -> s p e", e=2)


def tile_attend_ropemerge_kernel(tc, query, keys, cosn, sinn, ka, kb, offs, offs2, offs3, out):
    nc = tc.nc
    with ExitStack() as ctx:
        lists = ctx.enter_context(tc.tile_pool(name="lists", bufs=1))
        sb = ctx.enter_context(tc.tile_pool(name="sb", bufs=1))
        ps = ctx.enter_context(tc.psum_pool(name="ps", bufs=1))

        def bank(n):
            return ps.tile([P, BANK], F32, tag="bank%d" % n, name="bank%d" % n)

        def turn(dst, src, start, stop):
            nc.tensor.matmul(dst, lhsT=src, rhs=ident[:], is_transpose=True, start=start, stop=stop)

        list1 = lists.tile([P, I // 16], U16, name="list1")
        list2 = lists.tile([P, I // 16], U16, name="list2")
        list3 = lists.tile([P, I // 16], U16, name="list3")
        key_plane = [sb.tile([P, T], F32, name="key_plane%d" % t) for t in range(PLANES)]
        cos_rows = [sb.tile([P, U], F32, name="cos_rows%d" % u) for u in range(2)]
        sin_rows = [sb.tile([P, U], F32, name="sin_rows%d" % u) for u in range(2)]
        query_raw = sb.tile([P, PLANES, Q], F32, name="query_raw")
        keys_by_plane = keys.rearrange("(p t) n -> p t n", t=PLANES)
        cos_by_plane = cosn.rearrange("(p t) n -> p t n", t=PLANES)
        sin_by_plane = sinn.rearrange("(p t) n -> p t n", t=PLANES)

        share_rows = sb.tile([P, P], F32, name="share_rows")
        nc.vector.memset(share_rows[:], 0.0)
        nc.scalar.dma_start(out=share_rows[0:BLOCKS, :], in_=ka.rearrange("o (j p) -> (o j) p", p=P))
        nc.scalar.dma_start(out=share_rows[BLOCKS : 2 * BLOCKS, :], in_=kb.rearrange("o (j p) -> (o j) p", p=P))

        nc.sync.dma_start(list2[:], offs2)
        nc.sync.dma_start(out=key_plane[0][:], in_=keys_by_plane[:, 0, :])
        nc.sync.dma_start(list3[:], offs3)
        nc.sync.dma_start(out=cos_rows[0][:], in_=cos_by_plane[:, 0, :])
        nc.sync.dma_start(out=key_plane[1][:], in_=keys_by_plane[:, 1, :])
        nc.sync.dma_start(out=sin_rows[0][:], in_=sin_by_plane[:, 0, :])
        nc.sync.dma_start(out=key_plane[2][:], in_=keys_by_plane[:, 2, :])
        nc.sync.dma_start(out=cos_rows[1][:], in_=cos_by_plane[:, 2, :])
        nc.sync.dma_start(out=key_plane[3][:], in_=keys_by_plane[:, 3, :])
        nc.sync.dma_start(out=sin_rows[1][:], in_=sin_by_plane[:, 2, :])
        nc.sync.dma_start(list1[:], offs)
        nc.sync.dma_start(out=query_raw[:], in_=query.rearrange("(p t) q -> p t q", t=PLANES))

        ident = sb.tile([P, P], F32, name="ident")
        make_identity(nc, ident[:])

        share_turned = bank(6)
        turn(share_turned[:, 0:P], share_rows[:], True, True)
        share = sb.tile([P, 2 * BLOCKS], F32, name="share")
        nc.scalar.copy(out=share[:], in_=share_turned[:, 0 : 2 * BLOCKS])

        km16 = [sb.tile([P, HALF, PLANES], BF16, name="km16_%d" % h, align_bytes=64) for h in range(2)]
        query16 = sb.tile([P, Q, PLANES], BF16, name="query16", align_bytes=64)

        rotated = {}
        for u in range(2):
            second = sb.tile([P, 3, I], F32, name="second%d" % u)
            cos = sb.tile([P, I], F32, name="cos%d" % u)
            sin = sb.tile([P, I], F32, name="sin%d" % u)
            by_cos = sb.tile([P, 2, I], F32, name="by_cos%d" % u)
            by_sin = [sb.tile([P, 2, HALF], F32, name="by_sin%d_%d" % (u, h)) for h in range(2)]
            nc.vector.tensor_copy(second[:, 1, :], key_plane[2 * u][:].indirect(list2[:]))
            nc.vector.tensor_copy(cos[:], cos_rows[u][:].indirect(list3[:]))
            nc.vector.tensor_copy(second[:, 2, :], key_plane[2 * u + 1][:].indirect(list2[:]))
            nc.vector.tensor_copy(sin[:], sin_rows[u][:].indirect(list3[:]))
            nc.scalar.activation(out=second[:, 0, :], in_=second[:, 2, :], func=ACT.Copy, scale=-1.0)
            for e in range(2):
                nc.gpsimd.tensor_tensor(by_cos[:, e, :], second[:, 1 + e, :], cos[:], ALU.mult)
            for h in range(2):
                slots = slice(h * HALF, (h + 1) * HALF)
                sin_both = sin[:, slots].unsqueeze(1).to_broadcast([P, 2, HALF])
                nc.gpsimd.tensor_tensor(by_sin[h][:], second[:, 0:2, slots], sin_both, ALU.mult)
            k2_turned = [bank(2 * u + h) for h in range(2)]
            for e in range(2):
                for j in range(BLOCKS):
                    h, jj = divmod(j, 2)
                    turn(k2_turned[h][:, cols(2 * jj + e)], by_cos[:, e, cols(j)], e == 0 and jj == 0, False)
            for h in range(2):
                for e in range(2):
                    for jj in range(2):
                        turn(k2_turned[h][:, cols(2 * jj + e)], by_sin[h][:, e, cols(jj)], False, e == 1 and jj == 1)
                for jj in range(2):
                    j = 2 * h + jj
                    tag = "rotated%d_%d" % (u, j)
                    rotated[u, j] = sb.tile([P, P, 2], F32, name=tag, tag=tag, align_bytes=64)
                    nc.scalar.activation(
                        out=rotated[u, j][:],
                        in_=by_feature(k2_turned[h], jj),
                        func=ACT.Copy,
                        scale=share[:, BLOCKS + j : BLOCKS + j + 1],
                    )

        nc.scalar.copy(
            out=query16[:].rearrange("p (c i) t -> p c t i", i=RUN),
            in_=query_raw[:].rearrange("p t (c i) -> p c t i", i=RUN),
        )

        k1_turned = {}
        for u in range(2):
            first = sb.tile([P, 2, I], F32, name="first%d" % u)
            for h in range(2):
                k1_turned[u, h] = bank(4 - 2 * u + h)
            for e in range(2):
                nc.vector.tensor_copy(first[:, e, :], key_plane[2 * u + e][:].indirect(list1[:]))
                for j in range(BLOCKS):
                    h, jj = divmod(j, 2)
                    turn(k1_turned[u, h][:, cols(2 * jj + e)], first[:, e, cols(j)], True, True)

        words = [bank(n) for n in (0, 1, 6, 7)]
        for u in range(2):
            for j in range(BLOCKS):
                h, jj = divmod(j, 2)
                merged = sb.tile([P, P, 2], BF16, name="merged%d_%d" % (u, j))
                nc.vector.scalar_tensor_tensor(
                    merged[:], by_feature(k1_turned[u, h], jj), share[:, j : j + 1], rotated[u, j][:], ALU.mult, ALU.add
                )
                turn(words[j][:, cols(u)], merged[:].rearrange("s p e -> s (p e)").bitcast(F32), True, True)
        for j in range(BLOCKS):
            h, jj = divmod(j, 2)
            block16 = km16[h][:, cols(jj), :].rearrange("p s t -> p (s t)")
            nc.scalar.copy(
                out=block16.bitcast(F32).rearrange("p (s u) -> p s u", u=2),
                in_=words[j][:, 0 : 2 * P].rearrange("p (u s) -> p s u", u=2),
            )

        query_codes = sb.tile([P, Q], U32, name="query_codes", tag="rotated1_%d" % (BLOCKS - 1), align_bytes=64)
        query_scales = sb.tile([P, Q], U8, name="query_scales", align_bytes=64)
        nc.vector.quantize_mx(
            out=query_codes[:].bitcast(FP8X4), scales=query_scales[:], in_=query16[:].rearrange("p s t -> p (s t)")
        )
        km_codes = [sb.tile([P, HALF], U32, name="km_codes%d" % h, align_bytes=64) for h in range(2)]
        km_scales = [sb.tile([P, HALF], U8, name="km_scales%d" % h, align_bytes=64) for h in range(2)]
        for h in range(2):
            nc.vector.quantize_mx(
                out=km_codes[h][:].bitcast(FP8X4), scales=km_scales[h][:], in_=km16[h][:].rearrange("p s t -> p (s t)")
            )

        score = [bank(4 + m) for m in range(Q // P)]
        for h in range(2):
            for m in range(Q // P):
                nc.tensor.matmul_mx(
                    out=score[m][:, h * HALF : (h + 1) * HALF],
                    lhsT=query_codes[:, cols(m)].bitcast(FP8X4),
                    lhsT_scale=query_scales[:, cols(m)],
                    rhs=km_codes[h][:].bitcast(FP8X4),
                    rhs_scale=km_scales[h][:],
                    start=True,
                    stop=True,
                )

        for m in range(Q // P):
            neg_max = sb.tile([P, 1], F32, name="neg_max%d" % m)
            nc.vector.tensor_reduce(out=neg_max[:], in_=score[m][:], axis=mybir.AxisListType.X, op=ALU.max, negate=True)
            weight = sb.tile([P, I], F32, name="weight%d" % m)
            total = sb.tile([P, 1], F32, name="total%d" % m)
            nc.scalar.activation(
                out=weight[:], in_=score[m][:], func=ACT.Exp, bias=neg_max[:], scale=1.0, accum_out=total[:]
            )
            inverse = sb.tile([P, 1], F32, name="inverse%d" % m)
            nc.vector.reciprocal(out=inverse[:], in_=total[:])
            result = sb.tile([P, I], F32, name="result%d" % m)
            nc.vector.tensor_scalar(
                out=result[:], in0=weight[:], scalar1=inverse[:], scalar2=512.0, op0=ALU.mult, op1=ALU.mult
            )
            nc.sync.dma_start(out=out[cols(m), :], in_=result[:])
